import numpy as np
import ml_dtypes


def mxq(x, axis, fmt="e4m3"):
    dtype, down = {"e4m3": (ml_dtypes.float8_e4m3fn, 7), "e5m2": (ml_dtypes.float8_e5m2, 14)}[fmt]
    v = np.moveaxis(np.asarray(x, np.float32).astype(ml_dtypes.bfloat16).astype(np.float64), axis, -1)
    blocks = v.reshape(v.shape[:-1] + (-1, 32))
    amax = np.abs(blocks).max(-1, keepdims=True)
    byte = np.maximum(np.where(amax > 0, np.frexp(amax)[1] - 1 + 127, 0) - down, 1)
    scale = np.exp2(byte - 127.0)
    codes = (blocks / scale).astype(np.float32).astype(dtype).astype(np.float64)
    return np.moveaxis((codes * scale).reshape(v.shape), -1, axis)


WIDE = False


def mx_kscale(k):
    if not WIDE:
        return np.ones(k)
    levels = np.array([10, -10, 5, -5, 0])
    if k % 512:
        return np.exp2(np.random.permutation(np.resize(levels, k // 32))).repeat(32)
    a = np.empty((k // 512, 16))
    for p in range(k // 512):
        a[p, :8] = np.random.permutation(np.resize(levels, 8))
        for g in range(8):
            far = levels[np.abs(levels - a[p, g]) >= 10]
            a[p, g + 8] = far[np.random.randint(len(far))]
    return np.exp2(a.ravel()).repeat(32)


def f64(x):
    return np.asarray(x).astype(np.float64)


def striped(idx):
    return np.tile(idx.reshape(-1, 16).T, (8, 1)).astype(np.uint16)


def unstriped(offs):
    return offs[:16].T.reshape(-1).astype(np.int64)


def pack_weight(w):
    k, n = w.shape
    w = f64(np.asarray(w, np.float32).astype(ml_dtypes.bfloat16)).reshape(k // 32, 32, n)
    amax = np.abs(w).max(1)
    byte = np.clip(np.where(amax > 0, np.frexp(amax)[1] - 1 + 127 - 7, 1), 1, 254)
    scaled = (w * np.exp2(127.0 - byte)[:, None, :]).reshape(k, n).astype(np.float32)
    words = np.ascontiguousarray(scaled.reshape(k // 512, 128, 4, n).transpose(0, 1, 3, 2)).astype(ml_dtypes.float8_e4m3fn).view(np.uint8)
    return words, np.ascontiguousarray(byte.astype(np.uint8).reshape(k // 512, 16, n))


def unpack_weight(words, scales):
    g, p, n, _ = words.shape
    vals = np.ascontiguousarray(words).view(ml_dtypes.float8_e4m3fn).astype(np.float64) * np.repeat(np.exp2(scales.astype(np.float64) - 127.0), 8, axis=1)[..., None]
    return vals.transpose(0, 1, 3, 2).reshape(g * 512, n)


def relu(v):
    return np.maximum(v, 0.0)


K, T, S, D, N, V = 512, 2048, 1024, 4, 256, 256
P = 2 ** 7


def setup_inputs():
    n = np.random.standard_normal
    s = mx_kscale(K)[:, None]
    packed_xT = pack_weight(n((K, T)) * s)
    return {
        "x_words": packed_xT[0],
        "x_scales": packed_xT[1],
        "w1": (n((K, N)) / np.sqrt(K) / s).astype(np.float32),
        "w2": (n((K, N)) / np.sqrt(K) / s).astype(np.float32),
        "rad": (np.random.uniform(0.3, 1.2, (N, 1))).astype(np.float32),
        "fov": (np.tile(np.random.uniform(0.3, 1.0, S), (P, 1))).astype(np.float32),
        "want": (n((N, V))).astype(np.float32),
        "vel": (n((N, V))).astype(np.float32),
        "relax": (np.random.uniform(0.1, 0.6, (N, 1))).astype(np.float32),
        "offs": striped(np.random.permutation(T)[:S]),
    }


def reference(x_words, x_scales, w1, w2, rad, fov, want, vel, relax, offs):
    xq = unpack_weight(x_words, x_scales)[:, unstriped(offs)]
    y = mxq(f64(w1), 0, "e4m3").T @ xq
    z = mxq(f64(w2), 0, "e4m3").T @ xq
    ds = np.sqrt((y) ** 2 + (z) ** 2 + 0.1)
    st = (np.exp(-1.0 * ds + f64(rad))) * f64(fov)[:1]
    fx = (st * y) / ds
    ff = fx.reshape(len(fx), -1, D).sum(axis=2)
    nv = f64(vel) + f64(relax) * (f64(want) - f64(vel)) + 1.5 * ff
    return nv - relu(nv - 1.2) + relu(-1.0 * nv - 1.2)

@@ -1,0 +1,137 @@
+from contextlib import ExitStack
+
+import concourse.mybir as mybir
+
+K, T, S, D, N, V = 512, 2048, 1024, 4, 256, 256
+P = 128
+PACK = 4
+CHUNK = 512
+FLOPS = 2 * 2 * K * N * S
+
+F32 = mybir.dt.float32
+BF16 = mybir.dt.bfloat16
+I32 = mybir.dt.int32
+U32 = mybir.dt.uint32
+U16 = mybir.dt.uint16
+U8 = mybir.dt.uint8
+FP8X4 = mybir.dt.float8_e4m3fn_x4
+ALU = mybir.AluOpType
+ACT = mybir.ActivationFunctionType
+
+
+def tile_picked_ysocf_cap_p_kernel(tc, x_words, x_scales, w1, w2, rad, fov, want, vel, relax, offs, out):
+    nc = tc.nc
+    halves = S // CHUNK
+    blocks = N // P
+    chunks = [(b, h) for h in range(halves) for b in range(blocks)]
+    with ExitStack() as ctx:
+        keep = ctx.enter_context(tc.tile_pool(name="keep", bufs=1))
+        psum = ctx.enter_context(tc.psum_pool(name="psum", bufs=1))
+
+        def sbuf(name, shape, dtype):
+            return keep.tile(shape, dtype, name=name, align_bytes=64)
+
+        offsets = sbuf("offsets", [P, S // 16], U16)
+        nc.sync.dma_start(offsets[:], offs)
+
+        scale_table = sbuf("scale_table", [P, T], U8)
+        nc.vector.memset(scale_table[:].bitcast(I32), 0)
+        for q in range(4):
+            nc.scalar.dma_start(out=scale_table[32 * q : 32 * q + 4, :].bitcast(I32), in_=x_scales[0, 4 * q : 4 * q + 4, :].bitcast(I32))
+
+        warm_in = sbuf("warm_in", [P, 1], F32)
+        warm_out = sbuf("warm_out", [P, 1], F32)
+        nc.vector.memset(warm_in[:], 1.0)
+        nc.scalar.activation(out=warm_out[:], in_=warm_in[:], func=ACT.Abs_reciprocal_sqrt)
+
+        w_raw = [sbuf("w_raw%d" % i, [P, PACK, N], F32) for i in range(2)]
+        word_table = sbuf("word_table", [P, T], I32)
+        nc.sync.dma_start(out=w_raw[0][:], in_=w1.rearrange("(p j) m -> p j m", j=PACK))
+        nc.sync.dma_start(out=word_table[:], in_=x_words[0].rearrange("p c r -> p (c r)").bitcast(I32))
+        nc.sync.dma_start(out=w_raw[1][:], in_=w2.rearrange("(p j) m -> p j m", j=PACK))
+        fov_sb = sbuf("fov_sb", [P, S], F32)
+        nc.sync.dma_start(out=fov_sb[:], in_=fov)
+        want_sb = sbuf("want_sb", [P, blocks, V], F32)
+        vel_sb = sbuf("vel_sb", [P, blocks, V], F32)
+        nc.sync.dma_start(out=want_sb[:], in_=want.rearrange("(b p) v -> p b v", p=P))
+        nc.sync.dma_start(out=vel_sb[:], in_=vel.rearrange("(b p) v -> p b v", p=P))
+        rad_sb = sbuf("rad_sb", [P, blocks], F32)
+        relax_sb = sbuf("relax_sb", [P, blocks], F32)
+        with nc.allow_non_contiguous_dma(reason="one value a partition"):
+            nc.sync.dma_start(out=rad_sb[:], in_=rad.rearrange("(b p) o -> p (b o)", p=P))
+            nc.sync.dma_start(out=relax_sb[:], in_=relax.rearrange("(b p) o -> p (b o)", p=P))
+
+        def list_slice(h):
+            return offsets[:, h * (CHUNK // 16) : (h + 1) * (CHUNK // 16)]
+
+        x_scale = [sbuf("x_scale%d" % h, [P, CHUNK], U8) for h in range(halves)]
+        x_code = [sbuf("x_code%d" % h, [P, CHUNK], U32) for h in range(halves)]
+        w_code = [sbuf("w_code%d" % i, [P, N], U32) for i in range(2)]
+        w_scale = [sbuf("w_scale%d" % i, [P, N], U8) for i in range(2)]
+        w_bf = [sbuf("w_bf%d" % i, [P, N, PACK], BF16) for i in range(2)]
+
+        def round_weights(i):
+            nc.scalar.copy(out=w_bf[i][:], in_=w_raw[i][:].rearrange("p j m -> p m j"))
+
+        def quantise_weights(i):
+            nc.vector.quantize_mx(out=w_code[i][:].bitcast(FP8X4), scales=w_scale[i][:], in_=w_bf[i][:].rearrange("p m j -> p (m j)"))
+
+        def product(i, c):
+            b, h = chunks[c]
+            bank = psum.tile([P, CHUNK], F32, name="bank%d_%d" % (i, c))
+            cols = slice(b * P, (b + 1) * P)
+            nc.tensor.matmul_mx(out=bank[:], lhsT=w_code[i][:, cols].bitcast(FP8X4), lhsT_scale=w_scale[i][:, cols],
+                                rhs=x_code[h][:].bitcast(FP8X4), rhs_scale=x_scale[h][:], start=True, stop=True)
+            return bank
+
+        def per_chunk(name):
+            return [sbuf("%s%d" % (name, c), [P, CHUNK], F32) for c in range(len(chunks))]
+
+        y_sq, z_sq, dist_sq, inv_dist, dist, seen, pull, force = (
+            per_chunk(n) for n in ("y_sq", "z_sq", "dist_sq", "inv_dist", "dist", "seen", "pull", "force"))
+
+        for h in range(halves):
+            nc.vector.tensor_copy(out=x_scale[h][:], in_=scale_table[:].indirect(list_slice(h)))
+        round_weights(0)
+        quantise_weights(0)
+        for h in range(halves):
+            nc.vector.tensor_copy(out=x_code[h][:], in_=word_table[:].bitcast(U32).indirect(list_slice(h)))
+        y = [product(0, c) for c in range(len(chunks))]
+        round_weights(1)
+        quantise_weights(1)
+        z = [product(1, c) for c in range(len(chunks))]
+
+        for c, (b, h) in enumerate(chunks):
+            nc.scalar.activation(out=y_sq[c][:], in_=y[c][:], func=ACT.Square)
+            nc.vector.scalar_tensor_tensor(out=seen[c][:], in0=y[c][:], scalar=1.5, in1=fov_sb[:, h * CHUNK : (h + 1) * CHUNK], op0=ALU.mult, op1=ALU.mult)
+        for c in range(len(chunks)):
+            nc.scalar.activation(out=z_sq[c][:], in_=z[c][:], func=ACT.Square)
+            nc.vector.scalar_tensor_tensor(out=dist_sq[c][:], in0=y_sq[c][:], scalar=0.1, in1=z_sq[c][:], op0=ALU.add, op1=ALU.add)
+        for c in range(len(chunks)):
+            nc.scalar.activation(out=inv_dist[c][:], in_=dist_sq[c][:], func=ACT.Abs_reciprocal_sqrt)
+        for c in range(len(chunks)):
+            nc.vector.tensor_tensor(out=dist[c][:], in0=dist_sq[c][:], in1=inv_dist[c][:], op=ALU.mult)
+        for c in range(len(chunks)):
+            nc.vector.tensor_tensor(out=pull[c][:], in0=seen[c][:], in1=inv_dist[c][:], op=ALU.mult)
+
+        gap = sbuf("gap", [P, blocks, V], F32)
+        base = sbuf("base", [P, blocks, V], F32)
+        nc.vector.tensor_tensor(out=gap[:], in0=want_sb[:], in1=vel_sb[:], op=ALU.subtract)
+        for b in range(blocks):
+            nc.vector.scalar_tensor_tensor(out=base[:, b, :], in0=gap[:, b, :], scalar=relax_sb[:, b : b + 1], in1=vel_sb[:, b, :], op0=ALU.mult, op1=ALU.add)
+
+        last = len(chunks) - 1
+        strength = [y_sq[last], z_sq[last], y_sq[last - 1], z_sq[last - 1]]
+        walkers = CHUNK // D
+        for c, (b, h) in enumerate(chunks):
+            nc.scalar.activation(out=strength[c][:], in_=dist[c][:], func=ACT.Exp, scale=-1.0, bias=rad_sb[:, b : b + 1])
+        for c, (b, h) in enumerate(chunks):
+            nc.vector.tensor_tensor(out=force[c][:], in0=pull[c][:], in1=strength[c][:], op=ALU.mult)
+            total = sbuf("total%d" % c, [P, walkers], F32)
+            nc.vector.tensor_reduce(out=total[:], in_=force[c][:].rearrange("p (v d) -> p v d", d=D), axis=mybir.AxisListType.X, op=ALU.add)
+            cols = slice(h * walkers, (h + 1) * walkers)
+            speed = sbuf("speed%d" % c, [P, walkers], F32)
+            nc.vector.tensor_tensor(out=speed[:], in0=total[:], in1=base[:, b, cols], op=ALU.add)
+            capped = sbuf("capped%d" % c, [P, walkers], F32)
+            nc.vector.tensor_scalar(out=capped[:], in0=speed[:], scalar1=1.2, scalar2=-1.2, op0=ALU.min, op1=ALU.max)
+            nc.sync.dma_start(out=out[b * P : (b + 1) * P, cols], in_=capped[:])

@@ -1,6 +1,7 @@
 from contextlib import ExitStack
 
 import concourse.mybir as mybir
+from concourse.masks import make_identity
 
 K, T, S, D, N, V = 512, 2048, 1024, 4, 256, 256
 P = 128
@@ -35,31 +36,40 @@ def tile_picked_ysocf_cap_p_kernel(tc, x_words, x_scales, w1, w2, rad, fov, want
         nc.sync.dma_start(offsets[:], offs)
 
         scale_table = sbuf("scale_table", [P, T], U8)
-        nc.vector.memset(scale_table[:].bitcast(I32), 0)
-        for q in range(4):
-            nc.scalar.dma_start(out=scale_table[32 * q : 32 * q + 4, :].bitcast(I32), in_=x_scales[0, 4 * q : 4 * q + 4, :].bitcast(I32))
-
+        nc.gpsimd.memset(scale_table[:].bitcast(I32), 0)
         warm_in = sbuf("warm_in", [P, 1], F32)
         warm_out = sbuf("warm_out", [P, 1], F32)
         nc.vector.memset(warm_in[:], 1.0)
         nc.scalar.activation(out=warm_out[:], in_=warm_in[:], func=ACT.Abs_reciprocal_sqrt)
+        identity = sbuf("identity", [P, P], F32)
+        make_identity(nc, identity[:])
 
         w_raw = [sbuf("w_raw%d" % i, [P, PACK, N], F32) for i in range(2)]
         word_table = sbuf("word_table", [P, T], I32)
+        fov_col = sbuf("fov_col", [P, halves, D], F32)
+        with nc.allow_non_contiguous_dma(reason="a few values a partition"):
+            nc.sync.dma_start(out=fov_col[:], in_=fov[0].rearrange("(h v d) -> v h d", h=halves, d=D))
+        for q in range(4):
+            nc.sync.dma_start(out=scale_table[32 * q : 32 * q + 4, :].bitcast(I32), in_=x_scales[0, 4 * q : 4 * q + 4, :].bitcast(I32))
         nc.sync.dma_start(out=w_raw[0][:], in_=w1.rearrange("(p j) m -> p j m", j=PACK))
         nc.sync.dma_start(out=word_table[:], in_=x_words[0].rearrange("p c r -> p (c r)").bitcast(I32))
         nc.sync.dma_start(out=w_raw[1][:], in_=w2.rearrange("(p j) m -> p j m", j=PACK))
-        fov_sb = sbuf("fov_sb", [P, S], F32)
-        nc.sync.dma_start(out=fov_sb[:], in_=fov)
         want_sb = sbuf("want_sb", [P, blocks, V], F32)
         vel_sb = sbuf("vel_sb", [P, blocks, V], F32)
-        nc.sync.dma_start(out=want_sb[:], in_=want.rearrange("(b p) v -> p b v", p=P))
-        nc.sync.dma_start(out=vel_sb[:], in_=vel.rearrange("(b p) v -> p b v", p=P))
         rad_sb = sbuf("rad_sb", [P, blocks], F32)
         relax_sb = sbuf("relax_sb", [P, blocks], F32)
-        with nc.allow_non_contiguous_dma(reason="one value a partition"):
-            nc.sync.dma_start(out=rad_sb[:], in_=rad.rearrange("(b p) o -> p (b o)", p=P))
+        with nc.allow_non_contiguous_dma(reason="a few values a partition"):
             nc.sync.dma_start(out=relax_sb[:], in_=relax.rearrange("(b p) o -> p (b o)", p=P))
+            nc.sync.dma_start(out=want_sb[:], in_=want.rearrange("(b p) v -> p b v", p=P))
+            nc.sync.dma_start(out=vel_sb[:], in_=vel.rearrange("(b p) v -> p b v", p=P))
+            nc.sync.dma_start(out=rad_sb[:], in_=rad.rearrange("(b p) o -> p (b o)", p=P))
+
+        fov_wide = [sbuf("fov_wide%d" % h, [P, D, P], F32) for h in range(halves)]
+        for h in range(halves):
+            spread = psum.tile([P, D, P], F32, name="spread%d" % h, tag="z%d" % (2 + h))
+            for d in range(D):
+                nc.tensor.transpose(spread[:, d, :], fov_col[:, h, d : d + 1].to_broadcast([P, P]), identity[:])
+            nc.scalar.activation(out=fov_wide[h][:], in_=spread[:], func=ACT.Copy, scale=1.5)
 
         def list_slice(h):
             return offsets[:, h * (CHUNK // 16) : (h + 1) * (CHUNK // 16)]
@@ -78,14 +88,14 @@ def tile_picked_ysocf_cap_p_kernel(tc, x_words, x_scales, w1, w2, rad, fov, want
 
         def product(i, c):
             b, h = chunks[c]
-            bank = psum.tile([P, CHUNK], F32, name="bank%d_%d" % (i, c))
+            bank = psum.tile([P, CHUNK], F32, name="bank%d_%d" % (i, c), tag="%s%d" % ("yz"[i], c))
             cols = slice(b * P, (b + 1) * P)
             nc.tensor.matmul_mx(out=bank[:], lhsT=w_code[i][:, cols].bitcast(FP8X4), lhsT_scale=w_scale[i][:, cols],
                                 rhs=x_code[h][:].bitcast(FP8X4), rhs_scale=x_scale[h][:], start=True, stop=True)
-            return bank
+            return bank[:].rearrange("p (v d) -> p d v", d=D)
 
         def per_chunk(name):
-            return [sbuf("%s%d" % (name, c), [P, CHUNK], F32) for c in range(len(chunks))]
+            return [sbuf("%s%d" % (name, c), [P, D, P], F32) for c in range(len(chunks))]
 
         y_sq, z_sq, dist_sq, inv_dist, dist, seen, pull, force = (
             per_chunk(n) for n in ("y_sq", "z_sq", "dist_sq", "inv_dist", "dist", "seen", "pull", "force"))
@@ -102,10 +112,10 @@ def tile_picked_ysocf_cap_p_kernel(tc, x_words, x_scales, w1, w2, rad, fov, want
         z = [product(1, c) for c in range(len(chunks))]
 
         for c, (b, h) in enumerate(chunks):
-            nc.scalar.activation(out=y_sq[c][:], in_=y[c][:], func=ACT.Square)
-            nc.vector.scalar_tensor_tensor(out=seen[c][:], in0=y[c][:], scalar=1.5, in1=fov_sb[:, h * CHUNK : (h + 1) * CHUNK], op0=ALU.mult, op1=ALU.mult)
+            nc.scalar.activation(out=y_sq[c][:], in_=y[c], func=ACT.Square)
+            nc.vector.tensor_tensor(out=seen[c][:], in0=y[c], in1=fov_wide[h][:], op=ALU.mult)
         for c in range(len(chunks)):
-            nc.scalar.activation(out=z_sq[c][:], in_=z[c][:], func=ACT.Square)
+            nc.scalar.activation(out=z_sq[c][:], in_=z[c], func=ACT.Square)
             nc.vector.scalar_tensor_tensor(out=dist_sq[c][:], in0=y_sq[c][:], scalar=0.1, in1=z_sq[c][:], op0=ALU.add, op1=ALU.add)
         for c in range(len(chunks)):
             nc.scalar.activation(out=inv_dist[c][:], in_=dist_sq[c][:], func=ACT.Abs_reciprocal_sqrt)
@@ -114,24 +124,29 @@ def tile_picked_ysocf_cap_p_kernel(tc, x_words, x_scales, w1, w2, rad, fov, want
         for c in range(len(chunks)):
             nc.vector.tensor_tensor(out=pull[c][:], in0=seen[c][:], in1=inv_dist[c][:], op=ALU.mult)
 
-        gap = sbuf("gap", [P, blocks, V], F32)
-        base = sbuf("base", [P, blocks, V], F32)
-        nc.vector.tensor_tensor(out=gap[:], in0=want_sb[:], in1=vel_sb[:], op=ALU.subtract)
+        stay = sbuf("stay", [P, blocks], F32)
+        nc.gpsimd.tensor_scalar(out=stay[:], in0=relax_sb[:], scalar1=-1.0, scalar2=1.0, op0=ALU.mult, op1=ALU.add)
+        wished = sbuf("wished", [P, blocks, V], F32)
+        kept = sbuf("kept", [P, blocks, V], F32)
         for b in range(blocks):
-            nc.vector.scalar_tensor_tensor(out=base[:, b, :], in0=gap[:, b, :], scalar=relax_sb[:, b : b + 1], in1=vel_sb[:, b, :], op0=ALU.mult, op1=ALU.add)
+            nc.gpsimd.tensor_scalar(out=wished[:, b, :], in0=want_sb[:, b, :], scalar1=relax_sb[:, b : b + 1], scalar2=0.0, op0=ALU.mult, op1=ALU.add)
+            nc.gpsimd.tensor_scalar(out=kept[:, b, :], in0=vel_sb[:, b, :], scalar1=stay[:, b : b + 1], scalar2=0.0, op0=ALU.mult, op1=ALU.add)
 
         last = len(chunks) - 1
         strength = [y_sq[last], z_sq[last], y_sq[last - 1], z_sq[last - 1]]
-        walkers = CHUNK // D
         for c, (b, h) in enumerate(chunks):
             nc.scalar.activation(out=strength[c][:], in_=dist[c][:], func=ACT.Exp, scale=-1.0, bias=rad_sb[:, b : b + 1])
         for c, (b, h) in enumerate(chunks):
             nc.vector.tensor_tensor(out=force[c][:], in0=pull[c][:], in1=strength[c][:], op=ALU.mult)
-            total = sbuf("total%d" % c, [P, walkers], F32)
-            nc.vector.tensor_reduce(out=total[:], in_=force[c][:].rearrange("p (v d) -> p v d", d=D), axis=mybir.AxisListType.X, op=ALU.add)
-            cols = slice(h * walkers, (h + 1) * walkers)
-            speed = sbuf("speed%d" % c, [P, walkers], F32)
-            nc.vector.tensor_tensor(out=speed[:], in0=total[:], in1=base[:, b, cols], op=ALU.add)
-            capped = sbuf("capped%d" % c, [P, walkers], F32)
-            nc.vector.tensor_scalar(out=capped[:], in0=speed[:], scalar1=1.2, scalar2=-1.2, op0=ALU.min, op1=ALU.max)
+            cols = slice(h * P, (h + 1) * P)
+            terms = [wished[:, b, cols], kept[:, b, cols]] + [force[c][:, d, :] for d in range(D)]
+            speed_t = psum.tile([P, P], F32, name="speed_t%d" % c, tag="y%d" % c)
+            for i, term in enumerate(terms):
+                nc.tensor.matmul(speed_t[:], lhsT=term, rhs=identity[:], is_transpose=True, start=(i == 0), stop=(i == len(terms) - 1))
+            capped_t = sbuf("capped_t%d" % c, [P, P], F32)
+            nc.vector.tensor_scalar(out=capped_t[:], in0=speed_t[:], scalar1=1.2, scalar2=-1.2, op0=ALU.min, op1=ALU.max)
+            capped_ps = psum.tile([P, P], F32, name="capped_ps%d" % c, tag="z%d" % c)
+            nc.tensor.transpose(capped_ps[:], capped_t[:], identity[:])
+            capped = sbuf("capped%d" % c, [P, P], F32)
+            nc.scalar.copy(out=capped[:], in_=capped_ps[:])
             nc.sync.dma_start(out=out[b * P : (b + 1) * P, cols], in_=capped[:])

@@ -111,17 +111,18 @@ def tile_picked_ysocf_cap_p_kernel(tc, x_words, x_scales, w1, w2, rad, fov, want
         quantise_weights(1)
         z = [product(1, c) for c in range(len(chunks))]
 
-        for c, (b, h) in enumerate(chunks):
+        for c in range(len(chunks)):
             nc.scalar.activation(out=y_sq[c][:], in_=y[c], func=ACT.Square)
+        for h in range(halves):
+            for c in range(blocks * h, blocks * (h + 1)):
+                nc.scalar.activation(out=z_sq[c][:], in_=z[c], func=ACT.Square)
+                nc.vector.scalar_tensor_tensor(out=dist_sq[c][:], in0=y_sq[c][:], scalar=0.1, in1=z_sq[c][:], op0=ALU.add, op1=ALU.add)
+            for c in range(blocks * h, blocks * (h + 1)):
+                nc.scalar.activation(out=inv_dist[c][:], in_=dist_sq[c][:], func=ACT.Abs_reciprocal_sqrt)
+        for c, (b, h) in enumerate(chunks):
             nc.vector.tensor_tensor(out=seen[c][:], in0=y[c], in1=fov_wide[h][:], op=ALU.mult)
         for c in range(len(chunks)):
-            nc.scalar.activation(out=z_sq[c][:], in_=z[c], func=ACT.Square)
-            nc.vector.scalar_tensor_tensor(out=dist_sq[c][:], in0=y_sq[c][:], scalar=0.1, in1=z_sq[c][:], op0=ALU.add, op1=ALU.add)
-        for c in range(len(chunks)):
-            nc.scalar.activation(out=inv_dist[c][:], in_=dist_sq[c][:], func=ACT.Abs_reciprocal_sqrt)
-        for c in range(len(chunks)):
             nc.vector.tensor_tensor(out=dist[c][:], in0=dist_sq[c][:], in1=inv_dist[c][:], op=ALU.mult)
-        for c in range(len(chunks)):
             nc.vector.tensor_tensor(out=pull[c][:], in0=seen[c][:], in1=inv_dist[c][:], op=ALU.mult)
 
         stay = sbuf("stay", [P, blocks], F32)
@@ -132,6 +133,8 @@ def tile_picked_ysocf_cap_p_kernel(tc, x_words, x_scales, w1, w2, rad, fov, want
             nc.gpsimd.tensor_scalar(out=wished[:, b, :], in0=want_sb[:, b, :], scalar1=relax_sb[:, b : b + 1], scalar2=0.0, op0=ALU.mult, op1=ALU.add)
             nc.gpsimd.tensor_scalar(out=kept[:, b, :], in0=vel_sb[:, b, :], scalar1=stay[:, b : b + 1], scalar2=0.0, op0=ALU.mult, op1=ALU.add)
 
+        base = sbuf("base", [P, blocks, V], F32)
+        nc.gpsimd.tensor_tensor(out=base[:], in0=wished[:], in1=kept[:], op=ALU.add)
         last = len(chunks) - 1
         strength = [y_sq[last], z_sq[last], y_sq[last - 1], z_sq[last - 1]]
         for c, (b, h) in enumerate(chunks):
@@ -139,7 +142,18 @@ def tile_picked_ysocf_cap_p_kernel(tc, x_words, x_scales, w1, w2, rad, fov, want
         for c, (b, h) in enumerate(chunks):
             nc.vector.tensor_tensor(out=force[c][:], in0=pull[c][:], in1=strength[c][:], op=ALU.mult)
             cols = slice(h * P, (h + 1) * P)
-            terms = [wished[:, b, cols], kept[:, b, cols]] + [force[c][:, d, :] for d in range(D)]
+            capped = sbuf("capped%d" % c, [P, P], F32)
+            if c == len(chunks) - 1:
+                twos = sbuf("twos", [P, 2, P], F32)
+                nc.vector.tensor_tensor(out=twos[:], in0=force[c][:, 0:2, :], in1=force[c][:, 2:4, :], op=ALU.add)
+                total = sbuf("total", [P, P], F32)
+                nc.vector.tensor_tensor(out=total[:], in0=twos[:, 0, :], in1=twos[:, 1, :], op=ALU.add)
+                speed = sbuf("speed", [P, P], F32)
+                nc.vector.tensor_tensor(out=speed[:], in0=total[:], in1=base[:, b, cols], op=ALU.add)
+                nc.vector.tensor_scalar(out=capped[:], in0=speed[:], scalar1=1.2, scalar2=-1.2, op0=ALU.min, op1=ALU.max)
+                nc.sync.dma_start(out=out[b * P : (b + 1) * P, cols], in_=capped[:])
+                continue
+            terms = [base[:, b, cols]] + [force[c][:, d, :] for d in range(D)]
             speed_t = psum.tile([P, P], F32, name="speed_t%d" % c, tag="y%d" % c)
             for i, term in enumerate(terms):
                 nc.tensor.matmul(speed_t[:], lhsT=term, rhs=identity[:], is_transpose=True, start=(i == 0), stop=(i == len(terms) - 1))
@@ -147,6 +161,5 @@ def tile_picked_ysocf_cap_p_kernel(tc, x_words, x_scales, w1, w2, rad, fov, want
             nc.vector.tensor_scalar(out=capped_t[:], in0=speed_t[:], scalar1=1.2, scalar2=-1.2, op0=ALU.min, op1=ALU.max)
             capped_ps = psum.tile([P, P], F32, name="capped_ps%d" % c, tag="z%d" % c)
             nc.tensor.transpose(capped_ps[:], capped_t[:], identity[:])
-            capped = sbuf("capped%d" % c, [P, P], F32)
             nc.scalar.copy(out=capped[:], in_=capped_ps[:])
             nc.sync.dma_start(out=out[b * P : (b + 1) * P, cols], in_=capped[:])

from contextlib import ExitStack

import concourse.mybir as mybir
from concourse.masks import make_identity

K, T, S, D, N, V = 512, 2048, 1024, 4, 256, 256
P = 128
PACK = 4
CHUNK = 512
FLOPS = 2 * 2 * K * N * S

F32 = mybir.dt.float32
BF16 = mybir.dt.bfloat16
I32 = mybir.dt.int32
U32 = mybir.dt.uint32
U16 = mybir.dt.uint16
U8 = mybir.dt.uint8
FP8X4 = mybir.dt.float8_e4m3fn_x4
ALU = mybir.AluOpType
ACT = mybir.ActivationFunctionType


def tile_picked_ysocf_cap_p_kernel(tc, x_words, x_scales, w1, w2, rad, fov, want, vel, relax, offs, out):
    nc = tc.nc
    halves = S // CHUNK
    blocks = N // P
    chunks = [(b, h) for h in range(halves) for b in range(blocks)]
    with ExitStack() as ctx:
        keep = ctx.enter_context(tc.tile_pool(name="keep", bufs=1))
        psum = ctx.enter_context(tc.psum_pool(name="psum", bufs=1))

        def sbuf(name, shape, dtype):
            return keep.tile(shape, dtype, name=name, align_bytes=64)

        offsets = sbuf("offsets", [P, S // 16], U16)
        nc.sync.dma_start(offsets[:], offs)

        scale_table = sbuf("scale_table", [P, T], U8)
        nc.gpsimd.memset(scale_table[:].bitcast(I32), 0)
        warm_in = sbuf("warm_in", [P, 1], F32)
        warm_out = sbuf("warm_out", [P, 1], F32)
        nc.vector.memset(warm_in[:], 1.0)
        nc.scalar.activation(out=warm_out[:], in_=warm_in[:], func=ACT.Abs_reciprocal_sqrt)
        identity = sbuf("identity", [P, P], F32)
        make_identity(nc, identity[:])

        w_raw = [sbuf("w_raw%d" % i, [P, PACK, N], F32) for i in range(2)]
        word_table = sbuf("word_table", [P, T], I32)
        fov_col = sbuf("fov_col", [P, halves, D], F32)
        with nc.allow_non_contiguous_dma(reason="a few values a partition"):
            nc.sync.dma_start(out=fov_col[:], in_=fov[0].rearrange("(h v d) -> v h d", h=halves, d=D))
        for q in range(4):
            nc.sync.dma_start(out=scale_table[32 * q : 32 * q + 4, :].bitcast(I32), in_=x_scales[0, 4 * q : 4 * q + 4, :].bitcast(I32))
        nc.sync.dma_start(out=w_raw[0][:], in_=w1.rearrange("(p j) m -> p j m", j=PACK))
        nc.sync.dma_start(out=word_table[:], in_=x_words[0].rearrange("p c r -> p (c r)").bitcast(I32))
        nc.sync.dma_start(out=w_raw[1][:], in_=w2.rearrange("(p j) m -> p j m", j=PACK))
        want_sb = sbuf("want_sb", [P, blocks, V], F32)
        vel_sb = sbuf("vel_sb", [P, blocks, V], F32)
        rad_sb = sbuf("rad_sb", [P, blocks], F32)
        relax_sb = sbuf("relax_sb", [P, blocks], F32)
        with nc.allow_non_contiguous_dma(reason="a few values a partition"):
            nc.sync.dma_start(out=relax_sb[:], in_=relax.rearrange("(b p) o -> p (b o)", p=P))
            nc.sync.dma_start(out=want_sb[:], in_=want.rearrange("(b p) v -> p b v", p=P))
            nc.sync.dma_start(out=vel_sb[:], in_=vel.rearrange("(b p) v -> p b v", p=P))
            nc.sync.dma_start(out=rad_sb[:], in_=rad.rearrange("(b p) o -> p (b o)", p=P))

        fov_wide = [sbuf("fov_wide%d" % h, [P, D, P], F32) for h in range(halves)]
        for h in range(halves):
            spread = psum.tile([P, D, P], F32, name="spread%d" % h, tag="z%d" % (2 + h))
            for d in range(D):
                nc.tensor.transpose(spread[:, d, :], fov_col[:, h, d : d + 1].to_broadcast([P, P]), identity[:])
            nc.scalar.activation(out=fov_wide[h][:], in_=spread[:], func=ACT.Copy, scale=1.5)

        def list_slice(h):
            return offsets[:, h * (CHUNK // 16) : (h + 1) * (CHUNK // 16)]

        x_scale = [sbuf("x_scale%d" % h, [P, CHUNK], U8) for h in range(halves)]
        x_code = [sbuf("x_code%d" % h, [P, CHUNK], U32) for h in range(halves)]
        w_code = [sbuf("w_code%d" % i, [P, N], U32) for i in range(2)]
        w_scale = [sbuf("w_scale%d" % i, [P, N], U8) for i in range(2)]
        w_bf = [sbuf("w_bf%d" % i, [P, N, PACK], BF16) for i in range(2)]

        def round_weights(i):
            nc.scalar.copy(out=w_bf[i][:], in_=w_raw[i][:].rearrange("p j m -> p m j"))

        def quantise_weights(i):
            nc.vector.quantize_mx(out=w_code[i][:].bitcast(FP8X4), scales=w_scale[i][:], in_=w_bf[i][:].rearrange("p m j -> p (m j)"))

        def product(i, c):
            b, h = chunks[c]
            bank = psum.tile([P, CHUNK], F32, name="bank%d_%d" % (i, c), tag="%s%d" % ("yz"[i], c))
            cols = slice(b * P, (b + 1) * P)
            nc.tensor.matmul_mx(out=bank[:], lhsT=w_code[i][:, cols].bitcast(FP8X4), lhsT_scale=w_scale[i][:, cols],
                                rhs=x_code[h][:].bitcast(FP8X4), rhs_scale=x_scale[h][:], start=True, stop=True)
            return bank[:].rearrange("p (v d) -> p d v", d=D)

        def per_chunk(name):
            return [sbuf("%s%d" % (name, c), [P, D, P], F32) for c in range(len(chunks))]

        y_sq, z_sq, dist_sq, inv_dist, dist, seen, pull, force = (
            per_chunk(n) for n in ("y_sq", "z_sq", "dist_sq", "inv_dist", "dist", "seen", "pull", "force"))

        for h in range(halves):
            nc.vector.tensor_copy(out=x_scale[h][:], in_=scale_table[:].indirect(list_slice(h)))
        round_weights(0)
        quantise_weights(0)
        for h in range(halves):
            nc.vector.tensor_copy(out=x_code[h][:], in_=word_table[:].bitcast(U32).indirect(list_slice(h)))
        y = [product(0, c) for c in range(len(chunks))]
        round_weights(1)
        quantise_weights(1)
        z = [product(1, c) for c in range(len(chunks))]

        for c in range(len(chunks)):
            nc.scalar.activation(out=y_sq[c][:], in_=y[c], func=ACT.Square)
        for h in range(halves):
            for c in range(blocks * h, blocks * (h + 1)):
                nc.scalar.activation(out=z_sq[c][:], in_=z[c], func=ACT.Square)
                nc.vector.scalar_tensor_tensor(out=dist_sq[c][:], in0=y_sq[c][:], scalar=0.1, in1=z_sq[c][:], op0=ALU.add, op1=ALU.add)
            for c in range(blocks * h, blocks * (h + 1)):
                nc.scalar.activation(out=inv_dist[c][:], in_=dist_sq[c][:], func=ACT.Abs_reciprocal_sqrt)
        for c, (b, h) in enumerate(chunks):
            nc.vector.tensor_tensor(out=seen[c][:], in0=y[c], in1=fov_wide[h][:], op=ALU.mult)
        for c in range(len(chunks)):
            nc.vector.tensor_tensor(out=dist[c][:], in0=dist_sq[c][:], in1=inv_dist[c][:], op=ALU.mult)
            nc.vector.tensor_tensor(out=pull[c][:], in0=seen[c][:], in1=inv_dist[c][:], op=ALU.mult)

        stay = sbuf("stay", [P, blocks], F32)
        nc.gpsimd.tensor_scalar(out=stay[:], in0=relax_sb[:], scalar1=-1.0, scalar2=1.0, op0=ALU.mult, op1=ALU.add)
        wished = sbuf("wished", [P, blocks, V], F32)
        kept = sbuf("kept", [P, blocks, V], F32)
        for b in range(blocks):
            nc.gpsimd.tensor_scalar(out=wished[:, b, :], in0=want_sb[:, b, :], scalar1=relax_sb[:, b : b + 1], scalar2=0.0, op0=ALU.mult, op1=ALU.add)
            nc.gpsimd.tensor_scalar(out=kept[:, b, :], in0=vel_sb[:, b, :], scalar1=stay[:, b : b + 1], scalar2=0.0, op0=ALU.mult, op1=ALU.add)

        base = sbuf("base", [P, blocks, V], F32)
        nc.gpsimd.tensor_tensor(out=base[:], in0=wished[:], in1=kept[:], op=ALU.add)
        last = len(chunks) - 1
        strength = [y_sq[last], z_sq[last], y_sq[last - 1], z_sq[last - 1]]
        for c, (b, h) in enumerate(chunks):
            nc.scalar.activation(out=strength[c][:], in_=dist[c][:], func=ACT.Exp, scale=-1.0, bias=rad_sb[:, b : b + 1])
        for c, (b, h) in enumerate(chunks):
            nc.vector.tensor_tensor(out=force[c][:], in0=pull[c][:], in1=strength[c][:], op=ALU.mult)
            cols = slice(h * P, (h + 1) * P)
            capped = sbuf("capped%d" % c, [P, P], F32)
            if c == len(chunks) - 1:
                twos = sbuf("twos", [P, 2, P], F32)
                nc.vector.tensor_tensor(out=twos[:], in0=force[c][:, 0:2, :], in1=force[c][:, 2:4, :], op=ALU.add)
                total = sbuf("total", [P, P], F32)
                nc.vector.tensor_tensor(out=total[:], in0=twos[:, 0, :], in1=twos[:, 1, :], op=ALU.add)
                speed = sbuf("speed", [P, P], F32)
                nc.vector.tensor_tensor(out=speed[:], in0=total[:], in1=base[:, b, cols], op=ALU.add)
                nc.vector.tensor_scalar(out=capped[:], in0=speed[:], scalar1=1.2, scalar2=-1.2, op0=ALU.min, op1=ALU.max)
                nc.sync.dma_start(out=out[b * P : (b + 1) * P, cols], in_=capped[:])
                continue
            terms = [base[:, b, cols]] + [force[c][:, d, :] for d in range(D)]
            speed_t = psum.tile([P, P], F32, name="speed_t%d" % c, tag="y%d" % c)
            for i, term in enumerate(terms):
                nc.tensor.matmul(speed_t[:], lhsT=term, rhs=identity[:], is_transpose=True, start=(i == 0), stop=(i == len(terms) - 1))
            capped_t = sbuf("capped_t%d" % c, [P, P], F32)
            nc.vector.tensor_scalar(out=capped_t[:], in0=speed_t[:], scalar1=1.2, scalar2=-1.2, op0=ALU.min, op1=ALU.max)
            capped_ps = psum.tile([P, P], F32, name="capped_ps%d" % c, tag="z%d" % c)
            nc.tensor.transpose(capped_ps[:], capped_t[:], identity[:])
            nc.scalar.copy(out=capped[:], in_=capped_ps[:])
            nc.sync.dma_start(out=out[b * P : (b + 1) * P, cols], in_=capped[:])
